import numpy as np, ml_dtypes
CORES = [9,25,41,57]
N = 4
import mx_ref
BF = ml_dtypes.bfloat16
def entries(a):
    return np.ascontiguousarray(a.T).reshape(-1)
def table(e):
    return np.ascontiguousarray(np.reshape(e, (-1, 16)).T).astype(np.int32)
def gentries(a):
    return np.ascontiguousarray(a.reshape(8, 16, -1).transpose(0, 2, 1)).reshape(8, -1)
def gtable(e):
    e = np.asarray(e); return np.ascontiguousarray(e.reshape(8, -1, 16).transpose(0, 2, 1)).reshape(128, -1).astype(np.int32)
def cols(t, e):
    v = np.concatenate([t.reshape(128, -1, 4), np.zeros((128, 1, 4), BF)], axis=1)
    return np.ascontiguousarray(v[:, e]).reshape(128, -1)
def gpick(z, e):
    return np.concatenate([z[16 * g:16 * g + 16][:, e[g]] for g in range(8)])
def tile(rs):
    return np.stack(rs, axis=2).reshape(128, -1).astype(BF)
def cut(t, i, w=512):
    return t[:, w * i:w * i + w]
def f(rng, *shape):
    return mx_ref.flush((rng.standard_normal(shape, dtype=np.float32) * np.exp2(rng.integers(-2, 3, shape[:-1] + (1,)))).astype(BF))
def wide(rng, *shape, cols=0):
    v = rng.standard_normal(shape, dtype=np.float32) * np.exp2(rng.integers(-12, 13, shape)).astype(np.float32)
    if cols: v *= np.repeat(np.exp2(rng.integers(-cols, cols + 1, shape[:-2] + (1, shape[-1] // 4))) * (rng.random(shape[:-2] + (1, shape[-1] // 4)) > 0.0625), 4, axis=-1).astype(np.float32)
    return mx_ref.flush(v.astype(BF))
T, CAPP, KH, O = 512, 128, 512, 2
def lists(rng, kind="plain"):
    g = np.full((N, N * CAPP), -1)
    for s in range(N):
        for d in range(N):
            if d == s: continue
            n = rng.integers(0, CAPP + 1)
            if kind in ("foreign", "one"): n = CAPP
            if kind == "own": n = CAPP if d == (s + 1) % N else 0
            g[s, d * CAPP + rng.permutation(CAPP)[:n]] = rng.permutation(T)[:n] if n == CAPP else rng.integers(0, T, n)
    p = []
    for r in range(N):
        near = np.arange(T)
        far = T + np.flatnonzero(g[:, r * CAPP:(r + 1) * CAPP].reshape(-1) >= 0)
        if len(far) == 0: far = near
        e = np.where(rng.random((8, KH)) < 0.5, rng.choice(near, (8, KH)), rng.choice(far, (8, KH)))
        if kind == "agree": e = np.repeat(e[:1], 8, axis=0)
        if kind == "foreign": e = rng.choice(far, (8, KH))
        if kind == "own": e = rng.choice(near, (8, KH))
        if kind == "one":
            k = rng.permutation(np.concatenate([rng.permutation(near)[:4], rng.permutation(far)[:4]]))
            e = np.repeat(k[:, None], KH, axis=1)
        p.append(gtable(e))
    return {"snd": np.stack([table(g[s]) for s in range(N)]), "pk": np.stack(p)}
def setup_inputs(rng):
    return {"x": f(rng, N, 128, 4 * T), "w": f(rng, N, 128, 2048), "v": f(rng, N, 128, O * 512), **lists(rng)}
def setup_inputs_agree(rng):
    return {**setup_inputs(rng), **lists(rng, "agree")}
def setup_inputs_foreign(rng):
    return {**setup_inputs(rng), **lists(rng, "foreign")}
def setup_inputs_own(rng):
    return {**setup_inputs(rng), **lists(rng, "own")}
def setup_inputs_one(rng):
    return {**setup_inputs(rng), **lists(rng, "one")}
def setup_inputs_spread(rng):
    d = setup_inputs(rng); d["x"] = wide(rng, N, 128, 4 * T, cols=8); return d
def check_inputs(d):
    b = []
    g = np.stack([entries(d["snd"][s]) for s in range(N)])
    for r in range(N):
        if g[r].min() < -1 or g[r].max() >= T or (g[r, r * CAPP:(r + 1) * CAPP] != -1).any(): b.append("snd")
        e = gentries(d["pk"][r])
        if e.min() < 0 or e.max() >= T + N * CAPP: b.append("pk")
        else:
            used = g[:, r * CAPP:(r + 1) * CAPP].reshape(-1) >= 0
            if not used[e[e >= T] - T].all(): b.append("pk")
    return b
def reference(x, w, v, snd, pk):
    y = np.zeros((N, 128, O * KH), np.float32)
    for r in range(N):
        t = np.concatenate([x[r]] + [cols(x[s], entries(snd[s])[r * CAPP:(r + 1) * CAPP]) for s in range(N)], axis=1)
        q = mx_ref.quantize(np.ascontiguousarray(t))
        e = gentries(pk[r])
        rs = []
        for b in range(4):
            z = mx_ref.matmul(mx_ref.quantize(np.ascontiguousarray(cut(w[r], b))), q)
            rs.append(np.maximum(gpick(z, e), np.float32(0)) * np.float32(0.05))
        h = mx_ref.quantize(np.ascontiguousarray(tile(rs)))
        for o in range(O): y[r][:, KH * o:KH * o + KH] = mx_ref.matmul(mx_ref.quantize(np.ascontiguousarray(cut(v[r], o))), h)
    return {"y": y}

from concourse.mybir import dt, AluOpType, ActivationFunctionType

RELU = ActivationFunctionType.Relu
COPY = ActivationFunctionType.Copy

SCRATCH = {
    "sn": ("sbuf", [128, 32], "int32"),
    "pi": ("sbuf", [128, 32], "int32"),
    "po": ("sbuf", [128, 32], "uint16"),
    "xt": ("sbuf", [128, 2048], "bfloat16"),
    "wt": ("sbuf", [128, 2048], "bfloat16"),
    "vt": ("sbuf", [128, 1024], "bfloat16"),
    "xq": ("sbuf", [128, 512], "float8_e4m3fn_x4"),
    "xp": ("sbuf", [128, 512], "uint8"),
    "wq": ("sbuf", [128, 512], "float8_e4m3fn_x4"),
    "wp": ("sbuf", [128, 512], "uint8"),
    "vq": ("sbuf", [128, 256], "float8_e4m3fn_x4"),
    "vp": ("sbuf", [128, 256], "uint8"),
    "ht": ("sbuf", [128, 2048], "bfloat16"),
    "hq": ("sbuf", [128, 512], "float8_e4m3fn_x4"),
    "hp": ("sbuf", [128, 512], "uint8"),
    "ys": ("sbuf", [128, 1024], "float32"),
    "pa": ("psum", [128, 2048], "float32"),
    "pb": ("psum", [128, 2048], "float32"),
}
for _t in range(4):
    SCRATCH["of%d" % _t] = ("sbuf", [128, 32], "uint16")
    SCRATCH["z%d" % _t] = ("sbuf", [128, 1024], "float32")
for _j in range(3):
    SCRATCH["st%d" % _j] = ("sbuf", [128, 512], "bfloat16")
    SCRATCH["sq%d" % _j] = ("sbuf", [128, 128], "float8_e4m3fn_x4")
    SCRATCH["sp%d" % _j] = ("sbuf", [128, 128], "uint8")
    SCRATCH["lq%d" % _j] = ("sbuf", [128, 128], "float8_e4m3fn_x4")
    SCRATCH["lp%d" % _j] = ("sbuf", [128, 128], "uint8")

SEMAPHORES = ["sn", "xa", "xb", "w", "v", "pk", "mz", "off", "po", "qin", "qv", "sent", "yd", "ye"]
SEMAPHORES += ["g%d" % j for j in range(3)] + ["q%d" % j for j in range(3)] + ["arr%d" % j for j in range(3)]
SEMAPHORES += ["om%d" % b for b in range(4)] + ["oc%d" % b for b in range(4)]
SEMAPHORES += ["fm%d%d" % (j, b) for j in range(3) for b in range(4)] + ["fc%d%d" % (j, b) for j in range(3) for b in range(4)]
SEMAPHORES += ["hg%d" % c for c in range(2)] + ["hq%d" % c for c in range(2)]
SEMAPHORES += ["ym%d%d" % (c, o) for c in range(2) for o in range(2)] + ["yc%d%d" % (c, o) for c in range(2) for o in range(2)]

V_B, S_B = (0, 1), (2, 3)
ORDER = (0, 2, 1, 3)
HALVES = ((0, 256), (256, 512))


def rank_program(g, core, T, topo):
    rank = T.rank_of(core)
    if rank is None:
        return
    n_ranks = len(T.cores)
    t_cols, cap, kh = 512, 128, 512
    dests = [(rank + 1 + j) % n_ranks for j in range(n_ranks - 1)]
    froms = [(rank - 1 - j) % n_ranks for j in range(n_ranks - 1)]
    S = T.sem
    vec, sca, ten, syn = g.vector, g.scalar, g.tensor, g.sync

    syn.dma_start(T.xt[:, 0:1024], T.x[:, 0:1024]).then_inc(S.xa, 16)
    for i in range(4):
        sca.dma_start(T.sn[16 * i:16 * i + 16, :], T.snd[:, :]).then_inc(S.sn, 16)
    sca.dma_start(T.xt[:, 1024:2048], T.x[:, 1024:2048]).then_inc(S.xb, 16)
    sca.dma_start(T.wt[:, :], T.w[:, :]).then_inc(S.w, 16)
    sca.dma_start(T.pi[:, :], T.pk[:, :]).then_inc(S.pk, 16)
    syn.wait_ge(S.q1, 1)
    syn.dma_start(T.vt[:, :], T.v[:, :]).then_inc(S.v, 16)

    for b in range(4):
        a = t_cols + cap * rank
        vec.memset(T["z%d" % b][:, a:a + cap], 0.0).then_inc(S.mz, 1)
    vec.wait_ge(S.sn, 64)
    for t in range(4):
        for lo in (0, 64):
            vec.tensor_scalar(T["of%d" % t][lo:lo + 64, :], T.sn[0:64, :], 4.0, float(t), AluOpType.mult, AluOpType.add).then_inc(S.off, 1)
    vec.wait_ge(S.xa, 16)
    vec.quantize_mx(T.xq[:, 0:256], T.xp[:, 0:256], T.xt[:, 0:1024]).then_inc(S.qin, 1)

    for q in (vec, sca):
        q.wait_ge(S.off, 8)
        q.wait_ge(S.xa, 16)
        q.wait_ge(S.xb, 16)
    for j, d in enumerate(dests):
        a = d * cap // 16
        tile = T["st%d" % j]
        for t in V_B:
            vec.tensor_copy(tile[:, t:512:4], T.xt[:, 0:2048].indirect(T["of%d" % t][:, a:a + 8])).then_inc(S["g%d" % j], 1)
        for t in S_B:
            sca.activation(tile[:, t:512:4], T.xt[:, 0:2048].indirect(T["of%d" % t][:, a:a + 8]), COPY).then_inc(S["g%d" % j], 1)
        vec.wait_ge(S["g%d" % j], 4)
        vec.quantize_mx(T["sq%d" % j][:, :], T["sp%d" % j][:, :], tile[:, :]).then_inc(S["q%d" % j], 1)
        dst = T.cores[d]
        rid, pid, _ = topo.addr(dst)
        m = topo.mask(core, dst)
        g.wait_ge(S["q%d" % j], 1)
        g.remote_dma(T["lq%d" % j][:, :].bitcast(dt.uint8), T["sq%d" % j][:, :].bitcast(dt.uint8), S["arr%d" % j], S.sent, pid, rid, m)
        g.remote_dma(T["lp%d" % j][:, :], T["sp%d" % j][:, :], S["arr%d" % j], S.sent, pid, rid, m)
    incs = [2 * len(topo.engines(core, T.cores[d])) for d in dests]
    arr = [2 * len(topo.engines(T.cores[s], core)) for s in froms]
    g.wait_ge(S.sent, sum(incs))

    vec.quantize_mx(T.xq[:, 256:512], T.xp[:, 256:512], T.xt[:, 1024:2048]).then_inc(S.qin, 1)
    vec.wait_ge(S.w, 16)
    vec.quantize_mx(T.wq[:, :], T.wp[:, :], T.wt[:, :]).then_inc(S.qin, 1)
    vec.wait_ge(S.pk, 16)
    vec.tensor_copy(T.po[:, :], T.pi[:, :]).then_inc(S.po, 1)

    ten.wait_ge(S.qin, 3)
    for b in ORDER:
        ten.matmul_mx(T.pa[:, 512 * b:512 * b + 512], T.wq[:, 128 * b:128 * b + 128], T.wp[:, 128 * b:128 * b + 128],
                      T.xq[:, :], T.xp[:, :], True, True).then_inc(S["om%d" % b], 1)
    for b in V_B:
        vec.wait_ge(S["om%d" % b], 1)
        vec.tensor_copy(T["z%d" % b][:, 0:512], T.pa[:, 512 * b:512 * b + 512]).then_inc(S["oc%d" % b], 1)
    for b in S_B:
        sca.wait_ge(S["om%d" % b], 1)
        sca.activation(T["z%d" % b][:, 0:512], T.pa[:, 512 * b:512 * b + 512], COPY).then_inc(S["oc%d" % b], 1)
    vec.wait_ge(S.v, 16)
    vec.quantize_mx(T.vq[:, :], T.vp[:, :], T.vt[:, :]).then_inc(S.qv, 1)

    for j, s in enumerate(froms):
        ps = T.pb if j % 2 == 0 else T.pa
        ten.wait_ge(S["arr%d" % j], arr[j])
        for b in ORDER:
            if j == 1:
                ten.wait_ge(S["oc%d" % b], 1)
            if j == 2:
                ten.wait_ge(S["fc0%d" % b], 1)
            ten.matmul_mx(ps[:, 512 * b:512 * b + cap], T.wq[:, 128 * b:128 * b + 128], T.wp[:, 128 * b:128 * b + 128],
                          T["lq%d" % j][:, :], T["lp%d" % j][:, :], True, True).then_inc(S["fm%d%d" % (j, b)], 1)
        a = t_cols + cap * s
        for b in V_B:
            vec.wait_ge(S["fm%d%d" % (j, b)], 1)
            vec.tensor_copy(T["z%d" % b][:, a:a + cap], ps[:, 512 * b:512 * b + cap]).then_inc(S["fc%d%d" % (j, b)], 1)
        for b in S_B:
            sca.wait_ge(S["fm%d%d" % (j, b)], 1)
            sca.activation(T["z%d" % b][:, a:a + cap], ps[:, 512 * b:512 * b + cap], COPY).then_inc(S["fc%d%d" % (j, b)], 1)

    def ready(q, b):
        q.wait_ge(S["oc%d" % b], 1)
        for j in range(3):
            q.wait_ge(S["fc%d%d" % (j, b)], 1)

    def pick(c, b):
        lo, hi = HALVES[c]
        src = T["z%d" % b][:, 0:1024].indirect(T.po[:, lo // 16:hi // 16])
        out = T.ht[:, 4 * lo + b:4 * hi:4]
        if b in V_B:
            vec.tensor_scalar(out, src, 0.0, 0.05, AluOpType.max, AluOpType.mult).then_inc(S["hg%d" % c], 1)
        else:
            sca.activation(out, src, RELU, scale=0.05).then_inc(S["hg%d" % c], 1)

    def quant(c):
        lo, hi = HALVES[c]
        vec.wait_ge(S["hg%d" % c], 4)
        vec.quantize_mx(T.hq[:, lo:hi], T.hp[:, lo:hi], T.ht[:, 4 * lo:4 * hi]).then_inc(S["hq%d" % c], 1)

    def bank(c, o):
        lo, hi = HALVES[c]
        return T.pa[:, 512 * (2 * c + o):512 * (2 * c + o) + hi - lo]

    def out_of_psum(c, o):
        lo, hi = HALVES[c]
        out = T.ys[:, kh * o + lo:kh * o + hi]
        if o == 0:
            vec.wait_ge(S["ym%d%d" % (c, o)], 1)
            vec.tensor_copy(out, bank(c, o)).then_inc(S["yc%d%d" % (c, o)], 1)
        else:
            sca.wait_ge(S["ym%d%d" % (c, o)], 1)
            sca.activation(out, bank(c, o), COPY).then_inc(S["yc%d%d" % (c, o)], 1)

    def store(q, sem, c, o):
        lo, hi = HALVES[c]
        q.wait_ge(S["yc%d%d" % (c, o)], 1)
        q.dma_start(T.y[:, kh * o + lo:kh * o + hi], T.ys[:, kh * o + lo:kh * o + hi]).then_inc(sem, 16)

    for q in (vec, sca):
        q.wait_ge(S.mz, 4)
        q.wait_ge(S.po, 1)
    ten.wait_ge(S.qv, 1)
    for c in range(2):
        ten.wait_ge(S["hq%d" % c], 1)
        lo, hi = HALVES[c]
        for o in range(2):
            ten.wait_ge(S["fc1%d" % (2 * c + o)], 1)
            ten.matmul_mx(bank(c, o), T.vq[:, 128 * o:128 * o + 128], T.vp[:, 128 * o:128 * o + 128],
                          T.hq[:, lo:hi], T.hp[:, lo:hi], True, True).then_inc(S["ym%d%d" % (c, o)], 1)
    ready(vec, 0)
    pick(0, 0)
    ready(vec, 1)
    pick(0, 1)
    quant(0)
    pick(1, 0)
    out_of_psum(0, 0)
    pick(1, 1)
    quant(1)
    out_of_psum(1, 0)
    ready(sca, 2)
    pick(0, 2)
    ready(sca, 3)
    pick(0, 3)
    pick(1, 2)
    pick(1, 3)
    out_of_psum(0, 1)
    out_of_psum(1, 1)
    store(syn, S.yd, 0, 0)
    store(syn, S.yd, 0, 1)
    store(syn, S.yd, 1, 0)
    store(sca, S.ye, 1, 1)
    syn.wait_ge(S.yd, 48)
    sca.wait_ge(S.ye, 16)
